import numpy as np, ml_dtypes
CORES = [122,123,126,250,251,254,378,379,382,506,507,510]
N = 12
W, KW = 512, 5
H = KW // 2
def setup_inputs(rng):
    return {"x": rng.standard_normal((N, 128, W), dtype=np.float32).astype(ml_dtypes.bfloat16), "t": rng.standard_normal((N, 128, KW * W), dtype=np.float32).astype(ml_dtypes.bfloat16)}
def setup_inputs_big(rng):
    d = setup_inputs(rng)
    for k in ("x", "t"): d[k] = (d[k].astype(np.float32) * 1024.0).astype(d[k].dtype)
    return d
def setup_inputs_small(rng):
    d = setup_inputs(rng)
    for k in ("x", "t"): d[k] = (d[k].astype(np.float32) * (1 / 1024.0)).astype(d[k].dtype)
    return d
def reference(x, t):
    X, T = x.astype(np.float64), t.astype(np.float64)
    g = np.concatenate(list(X), axis=1)
    p = np.concatenate([g[:, -H:], g, g[:, :H]], axis=1)
    y = np.stack([sum(T[r][:, W * i:W * i + W] * p[:, W * r + i:W * r + i + W] for i in range(KW)) for r in range(N)])
    return {"y": y.astype(ml_dtypes.bfloat16 if x.dtype != np.float64 else np.float64)}

@@ -1,0 +1,112 @@
+from concourse.bass import DstId, RemoteDMATransfer
+from concourse.mybir import AluOpType
+
+W = 512
+ORDER = [2, 4, 0, 3, 1]
+
+SCRATCH = {
+    "edge": ("dram", [128, 4], "bfloat16"),
+    "land": ("dram", [2, 128, 4], "bfloat16"),
+    "hal": ("sbuf", [128, 4], "bfloat16"),
+    "xs": ("sbuf", [128, W], "bfloat16"),
+    "ts": ("sbuf", [128, 5 * W], "bfloat16"),
+    "pb": ("sbuf", [128, 5 * W], "bfloat16"),
+    "ysb": ("sbuf", [128, W], "bfloat16"),
+    "qa": ("sbuf", [128, 4], "float32"),
+    "qb": ("sbuf", [128, 2], "float32"),
+    "zz": ("sbuf", [128, 129], "bfloat16"),
+    "idd": ("dram", [1, 128 * 129], "bfloat16"),
+    "ident": ("sbuf", [128, 128], "bfloat16"),
+    "xp": ("psum", [128, W], "float32"),
+    "acc": ("psum", [128, W], "float32"),
+}
+SEMAPHORES = ["el", "sent", "arr", "hs", "xl", "tl0", "tl1", "tl2", "tl3", "tl4", "zs", "pz", "id1", "idl", "xc",
+              "pr0", "pr1", "pr2", "pr3", "pr4", "ad", "fin", "q", "q2", "ye", "st"]
+
+
+def rank_program(g, core, T, topo):
+    rank = T.rank_of(core)
+    if rank is None:
+        return
+    n = len(T.cores)
+    left, right = T.cores[(rank - 1) % n], T.cores[(rank + 1) % n]
+    S = T.sem
+    sy, sc, ve, pe = g.sync, g.scalar, g.vector, g.tensor
+    mult, add = AluOpType.mult, AluOpType.add
+
+    def load_table(q, k):
+        i = ORDER[k]
+        q.dma_start(T.ts[:, W * k:W * k + W], T.t[:, W * i:W * i + W]).then_inc(S["tl%d" % k], 16)
+
+    sy.dma_start(T.edge[:, 0:2], T.x[:, 0:2]).then_inc(S.el, 16)
+    sc.dma_start(T.edge[:, 2:4], T.x[:, W - 2:W]).then_inc(S.el, 16)
+    sy.dma_start(T.xs[:], T.x[:]).then_inc(S.xl, 16)
+    load_table(sy, 0)
+    sc.wait_ge(S.zs, 2)
+    sc.dma_start(T.idd[0], T.zz[:]).then_inc(S.id1, 16)
+    sy.wait_ge(S.zs, 2)
+    load_table(sc, 1)
+    load_table(sy, 2)
+    load_table(sc, 3)
+    load_table(sc, 4)
+    sy.wait_ge(S.id1, 16)
+    sy.dma_start(T.ident[:], T.idd[0, 0:128 * 128]).then_inc(S.idl, 16)
+
+    g.wait_ge(S.el, 32)
+    dests = [(left, T.land[1]), (right, T.land[0])]
+    here = (topo.host(core), topo.chip(core))
+    dests.sort(key=lambda d: (topo.host(d[0]), topo.chip(d[0])) == here)
+    allowed = topo.mask(core, left) & topo.mask(core, right)
+    engine = allowed & (-allowed)
+    ids = []
+    for d, _ in dests:
+        rid, pid = topo.addr(d, core)
+        ids.append(DstId(rid=rid, pnc=pid))
+    g.remote_dma_fused([RemoteDMATransfer(dst_ids=ids, dma_engine_mask=engine, remote_sem=S.arr,
+                                          srcs=[T.edge[:]], dsts=[ap for _, ap in dests], alu_op=0)],
+                       local_sem=S.sent)
+    g.wait_ge(S.sent, 1)
+
+    sy.wait_ge(S.arr, 2)
+    sy.dma_start(T.hal[:, 2:4], T.land[0, :, 2:4]).then_inc(S.hs, 16)
+    sc.wait_ge(S.arr, 2)
+    sc.dma_start(T.hal[:, 0:2], T.land[1, :, 0:2]).then_inc(S.hs, 16)
+
+    ve.memset(T.zz[:, 0:1], 1.0).then_inc(S.zs, 1)
+    ve.memset(T.zz[:, 1:129], 0.0).then_inc(S.zs, 1)
+    ve.memset(T.pb[:, 2 * W - 2:2 * W + 2], 0.0).then_inc(S.pz, 1)
+    ve.memset(T.pb[:, 4 * W - 1:4 * W + 1], 0.0).then_inc(S.pz, 1)
+    ve.wait_ge(S.xl, 16)
+    ve.tensor_copy(T.xp[:], T.xs[:]).then_inc(S.xc, 1)
+    ve.wait_ge(S.xc, 1)
+    for k in range(5):
+        d = ORDER[k] - 2
+        lo, hi = max(0, -d), min(W, W - d)
+        ve.wait_ge(S["tl%d" % k], 16)
+        ve.tensor_tensor(T.pb[:, W * k + lo:W * k + hi], T.ts[:, W * k + lo:W * k + hi], T.xp[:, lo + d:hi + d],
+                         mult).then_inc(S["pr%d" % k], 1)
+
+    pe.wait_ge(S.idl, 16)
+    pe.wait_ge(S.pz, 2)
+    for k in range(4):
+        pe.wait_ge(S["pr%d" % k], 1)
+        mm = pe.matmul(T.acc[:], T.ident[:], T.pb[:, W * k:W * k + W], k == 0, k == 3)
+    mm.then_inc(S.ad, 1)
+
+    ve.wait_ge(S.pz, 2)
+    ve.wait_ge(S.pr4, 1)
+    ve.wait_ge(S.ad, 1)
+    ve.tensor_tensor(T.ysb[:], T.acc[:], T.pb[:, 4 * W:5 * W], add).then_inc(S.fin, 1)
+    ve.wait_ge(S.hs, 32)
+    ve.tensor_tensor(T.qb[:], T.ts[:, 4 * W - 1:4 * W + 1], T.hal[:, 0:4:3], mult).then_inc(S.q, 1)
+    ve.tensor_tensor(T.qa[:], T.ts[:, 2 * W - 2:2 * W + 2], T.hal[:], mult).then_inc(S.q, 1)
+    ve.wait_ge(S.q, 2)
+    ve.tensor_tensor(T.qa[:, 1:3], T.qa[:, 1:3], T.qb[:], add).then_inc(S.q2, 1)
+    ve.wait_ge(S.q2, 1)
+    ve.wait_ge(S.fin, 1)
+    ve.tensor_tensor(T.ysb[:, W - 2:W], T.ysb[:, W - 2:W], T.qa[:, 0:2], add).then_inc(S.ye, 1)
+    ve.tensor_tensor(T.ysb[:, 0:2], T.ysb[:, 0:2], T.qa[:, 2:4], add).then_inc(S.ye, 1)
+
+    sy.wait_ge(S.ye, 2)
+    sy.dma_start(T.y[:], T.ysb[:]).then_inc(S.st, 16)
+    sy.wait_ge(S.st, 16)

@@ -1,27 +1,37 @@
 from concourse.bass import DstId, RemoteDMATransfer
-from concourse.mybir import AluOpType
+from concourse.mybir import AluOpType, ActivationFunctionType
 
 W = 512
+HW_ = W // 2
+C = W // 4
+R = 2
+NENG = 8
 ORDER = [2, 4, 0, 3, 1]
+LAST = [3, 0, 1, 2]
 
 SCRATCH = {
-    "edge": ("dram", [128, 4], "bfloat16"),
-    "land": ("dram", [2, 128, 4], "bfloat16"),
-    "hal": ("sbuf", [128, 4], "bfloat16"),
+    "eg": ("sbuf", [128, 4], "bfloat16"),
+    "hal8": ("sbuf", [128, 8], "bfloat16"),
     "xs": ("sbuf", [128, W], "bfloat16"),
     "ts": ("sbuf", [128, 5 * W], "bfloat16"),
     "pb": ("sbuf", [128, 5 * W], "bfloat16"),
     "ysb": ("sbuf", [128, W], "bfloat16"),
+    "ye4": ("sbuf", [128, 4], "bfloat16"),
     "qa": ("sbuf", [128, 4], "float32"),
     "qb": ("sbuf", [128, 2], "float32"),
-    "zz": ("sbuf", [128, 129], "bfloat16"),
-    "idd": ("dram", [1, 128 * 129], "bfloat16"),
+    "ones": ("sbuf", [128, 128], "bfloat16"),
     "ident": ("sbuf", [128, 128], "bfloat16"),
-    "xp": ("psum", [128, W], "float32"),
-    "acc": ("psum", [128, W], "float32"),
+    "xa": ("psum", [128, W], "float32"),
+    "xb": ("psum", [128, W], "float32"),
+    "acc0": ("psum", [128, W], "float32"),
+    "acc1": ("psum", [128, W], "float32"),
+    "acc2": ("psum", [128, W], "float32"),
+    "acc3": ("psum", [128, W], "float32"),
 }
-SEMAPHORES = ["el", "sent", "arr", "hs", "xl", "tl0", "tl1", "tl2", "tl3", "tl4", "zs", "pz", "id1", "idl", "xc",
-              "pr0", "pr1", "pr2", "pr3", "pr4", "ad", "fin", "q", "q2", "ye", "st"]
+SEMAPHORES = (["el", "sent", "arr", "xl", "on", "pz", "idl", "xca", "xcb", "q", "q2", "yes", "sts", "sty"]
+              + ["tl%d" % k for k in range(5)]
+              + ["pr%d%d" % (k, h) for k in range(4) for h in range(2)]
+              + ["pl%d" % j for j in range(4)] + ["ad%d" % j for j in range(4)] + ["ev%d" % j for j in range(4)])
 
 
 def rank_program(g, core, T, topo):
@@ -33,80 +43,115 @@ def rank_program(g, core, T, topo):
     S = T.sem
     sy, sc, ve, pe = g.sync, g.scalar, g.vector, g.tensor
     mult, add = AluOpType.mult, AluOpType.add
+    copy = ActivationFunctionType.Copy
 
     def load_table(q, k):
         i = ORDER[k]
         q.dma_start(T.ts[:, W * k:W * k + W], T.t[:, W * i:W * i + W]).then_inc(S["tl%d" % k], 16)
 
-    sy.dma_start(T.edge[:, 0:2], T.x[:, 0:2]).then_inc(S.el, 16)
-    sc.dma_start(T.edge[:, 2:4], T.x[:, W - 2:W]).then_inc(S.el, 16)
-    sy.dma_start(T.xs[:], T.x[:]).then_inc(S.xl, 16)
-    load_table(sy, 0)
-    sc.wait_ge(S.zs, 2)
-    sc.dma_start(T.idd[0], T.zz[:]).then_inc(S.id1, 16)
-    sy.wait_ge(S.zs, 2)
-    load_table(sc, 1)
-    load_table(sy, 2)
-    load_table(sc, 3)
-    load_table(sc, 4)
-    sy.wait_ge(S.id1, 16)
-    sy.dma_start(T.ident[:], T.idd[0, 0:128 * 128]).then_inc(S.idl, 16)
+    def ypos(j):
+        return (C * j + HW_) % W
 
+    sy.dma_start(T.eg[:, 2:4], T.x[:, 0:2]).then_inc(S.el, 16)
+    sc.dma_start(T.eg[:, 0:2], T.x[:, W - 2:W]).then_inc(S.el, 16)
+    sy.dma_start(T.xs[:], T.x[:]).then_inc(S.xl, 16)
+    load_table(sc, 0)
+    load_table(sy, 1)
+    load_table(sc, 2)
+    load_table(sy, 3)
+    load_table(sc, 4)
+
+    g.wait_ge(S.on, 1)
+    g.affine_select(T.ident[:], T.ones[:], [[-1, 128]], AluOpType.is_equal, 0.0, 0, 1).then_inc(S.idl, 1)
     g.wait_ge(S.el, 32)
-    dests = [(left, T.land[1]), (right, T.land[0])]
+    dests = [(left, T.hal8[:, 0:4]), (right, T.hal8[:, 4:8])]
     here = (topo.host(core), topo.chip(core))
     dests.sort(key=lambda d: (topo.host(d[0]), topo.chip(d[0])) == here)
     allowed = topo.mask(core, left) & topo.mask(core, right)
-    engine = allowed & (-allowed)
+    engines = 0
+    for _ in range(NENG):
+        rest = allowed & ~engines
+        engines |= rest & (-rest)
     ids = []
     for d, _ in dests:
         rid, pid = topo.addr(d, core)
         ids.append(DstId(rid=rid, pnc=pid))
-    g.remote_dma_fused([RemoteDMATransfer(dst_ids=ids, dma_engine_mask=engine, remote_sem=S.arr,
-                                          srcs=[T.edge[:]], dsts=[ap for _, ap in dests], alu_op=0)],
+    g.remote_dma_fused([RemoteDMATransfer(dst_ids=ids, dma_engine_mask=engines, remote_sem=S.arr,
+                                          srcs=[T.eg[:]], dsts=[ap for _, ap in dests], alu_op=0)],
                        local_sem=S.sent)
-    g.wait_ge(S.sent, 1)
+    g.wait_ge(S.sent, NENG)
 
-    sy.wait_ge(S.arr, 2)
-    sy.dma_start(T.hal[:, 2:4], T.land[0, :, 2:4]).then_inc(S.hs, 16)
-    sc.wait_ge(S.arr, 2)
-    sc.dma_start(T.hal[:, 0:2], T.land[1, :, 0:2]).then_inc(S.hs, 16)
+    pe.wait_ge(S.idl, 1)
+    pe.wait_ge(S.xl, 16)
+    pe.matmul(T.xa[:, 0:HW_ + R], T.ident[:], T.xs[:, 0:HW_ + R], True, True).then_inc(S.xca, 1)
+    sc.wait_ge(S.xl, 16)
+    sc.activation(T.xb[:, 0:HW_ + R], T.xs[:, HW_ - R:W], copy).then_inc(S.xcb, 1)
 
-    ve.memset(T.zz[:, 0:1], 1.0).then_inc(S.zs, 1)
-    ve.memset(T.zz[:, 1:129], 0.0).then_inc(S.zs, 1)
+    ve.memset(T.ones[:], 1.0).then_inc(S.on, 1)
     ve.memset(T.pb[:, 2 * W - 2:2 * W + 2], 0.0).then_inc(S.pz, 1)
     ve.memset(T.pb[:, 4 * W - 1:4 * W + 1], 0.0).then_inc(S.pz, 1)
-    ve.wait_ge(S.xl, 16)
-    ve.tensor_copy(T.xp[:], T.xs[:]).then_inc(S.xc, 1)
-    ve.wait_ge(S.xc, 1)
-    for k in range(5):
-        d = ORDER[k] - 2
-        lo, hi = max(0, -d), min(W, W - d)
-        ve.wait_ge(S["tl%d" % k], 16)
-        ve.tensor_tensor(T.pb[:, W * k + lo:W * k + hi], T.ts[:, W * k + lo:W * k + hi], T.xp[:, lo + d:hi + d],
-                         mult).then_inc(S["pr%d" % k], 1)
 
-    pe.wait_ge(S.idl, 16)
+    def product(k, c0, c1, sem):
+        d = ORDER[k] - R
+        lo, hi = max(c0, -d), min(c1, W - d)
+        if c0 < HW_:
+            xap = T.xa[:, lo + d:hi + d]
+        else:
+            off = HW_ - R
+            xap = T.xb[:, lo + d - off:hi + d - off]
+        ve.tensor_tensor(T.pb[:, W * k + lo:W * k + hi], T.ts[:, W * k + lo:W * k + hi], xap, mult).then_inc(sem, 1)
+
+    ve.wait_ge(S.xca, 1)
+    for k in range(4):
+        ve.wait_ge(S["tl%d" % k], 16)
+        product(k, 0, HW_, S["pr%d0" % k])
+        if k == 0:
+            ve.wait_ge(S.xcb, 1)
+        product(k, HW_, W, S["pr%d1" % k])
+    ve.wait_ge(S.tl4, 16)
+    for j in LAST:
+        product(4, C * j, C * j + C, S["pl%d" % j])
+
     pe.wait_ge(S.pz, 2)
     for k in range(4):
-        pe.wait_ge(S["pr%d" % k], 1)
-        mm = pe.matmul(T.acc[:], T.ident[:], T.pb[:, W * k:W * k + W], k == 0, k == 3)
-    mm.then_inc(S.ad, 1)
+        for h in range(2):
+            pe.wait_ge(S["pr%d%d" % (k, h)], 1)
+            for j in (2 * h, 2 * h + 1):
+                pe.matmul(T["acc%d" % j][:, 0:C], T.ident[:], T.pb[:, W * k + C * j:W * k + C * j + C], k == 0, False)
+    for j in LAST:
+        pe.wait_ge(S["pl%d" % j], 1)
+        pe.matmul(T["acc%d" % j][:, 0:C], T.ident[:], T.pb[:, W * 4 + C * j:W * 4 + C * j + C], False,
+                  True).then_inc(S["ad%d" % j], 1)
 
-    ve.wait_ge(S.pz, 2)
-    ve.wait_ge(S.pr4, 1)
-    ve.wait_ge(S.ad, 1)
-    ve.tensor_tensor(T.ysb[:], T.acc[:], T.pb[:, 4 * W:5 * W], add).then_inc(S.fin, 1)
-    ve.wait_ge(S.hs, 32)
-    ve.tensor_tensor(T.qb[:], T.ts[:, 4 * W - 1:4 * W + 1], T.hal[:, 0:4:3], mult).then_inc(S.q, 1)
-    ve.tensor_tensor(T.qa[:], T.ts[:, 2 * W - 2:2 * W + 2], T.hal[:], mult).then_inc(S.q, 1)
+    def evacuate(j):
+        sc.wait_ge(S["ad%d" % j], 1)
+        sc.activation(T.ysb[:, ypos(j):ypos(j) + C], T["acc%d" % j][:, 0:C], copy).then_inc(S["ev%d" % j], 1)
+
+    evacuate(3)
+    sc.wait_ge(S.ev3, 1)
+    sc.dma_start(T.y[:, 3 * C:W - R], T.ysb[:, ypos(3):ypos(3) + C - R]).then_inc(S.sts, 16)
+    evacuate(0)
+    evacuate(1)
+    sc.wait_ge(S.ev0, 1)
+    sc.wait_ge(S.ev1, 1)
+    sc.dma_start(T.y[:, R:2 * C], T.ysb[:, ypos(0) + R:ypos(0) + 2 * C]).then_inc(S.sts, 16)
+    evacuate(2)
+    sc.wait_ge(S.ev2, 1)
+    sc.dma_start(T.y[:, 2 * C:3 * C], T.ysb[:, ypos(2):ypos(2) + C]).then_inc(S.sts, 16)
+
+    ve.wait_ge(S.arr, 2 * NENG)
+    ve.tensor_tensor(T.qb[:], T.ts[:, 4 * W - 1:4 * W + 1], T.hal8[:, 2:6:3], mult).then_inc(S.q, 1)
+    ve.tensor_tensor(T.qa[:], T.ts[:, 2 * W - 2:2 * W + 2], T.hal8[:, 2:6], mult).then_inc(S.q, 1)
     ve.wait_ge(S.q, 2)
     ve.tensor_tensor(T.qa[:, 1:3], T.qa[:, 1:3], T.qb[:], add).then_inc(S.q2, 1)
     ve.wait_ge(S.q2, 1)
-    ve.wait_ge(S.fin, 1)
-    ve.tensor_tensor(T.ysb[:, W - 2:W], T.ysb[:, W - 2:W], T.qa[:, 0:2], add).then_inc(S.ye, 1)
-    ve.tensor_tensor(T.ysb[:, 0:2], T.ysb[:, 0:2], T.qa[:, 2:4], add).then_inc(S.ye, 1)
+    ve.wait_ge(S.ev3, 1)
+    ve.wait_ge(S.ev0, 1)
+    ve.tensor_tensor(T.ye4[:], T.ysb[:, HW_ - R:HW_ + R], T.qa[:], add).then_inc(S.yes, 1)
 
-    sy.wait_ge(S.ye, 2)
-    sy.dma_start(T.y[:], T.ysb[:]).then_inc(S.st, 16)
-    sy.wait_ge(S.st, 16)
+    sy.wait_ge(S.yes, 1)
+    sy.dma_start(T.y[:, W - R:W], T.ye4[:, 0:R]).then_inc(S.sty, 16)
+    sc.wait_ge(S.yes, 1)
+    sc.dma_start(T.y[:, 0:R], T.ye4[:, R:2 * R]).then_inc(S.sts, 16)
+    sy.wait_ge(S.sty, 16)
+    sc.wait_ge(S.sts, 64)

@@ -7,7 +7,8 @@ C = W // 4
 R = 2
 NENG = 8
 ORDER = [2, 4, 0, 3, 1]
-LAST = [3, 0, 1, 2]
+FIRST = 160
+GROUPS = [(3, 0), (1, 2)]
 
 SCRATCH = {
     "eg": ("sbuf", [128, 4], "bfloat16"),
@@ -17,7 +18,7 @@ SCRATCH = {
     "pb": ("sbuf", [128, 5 * W], "bfloat16"),
     "ysb": ("sbuf", [128, W], "bfloat16"),
     "ye4": ("sbuf", [128, 4], "bfloat16"),
-    "qa": ("sbuf", [128, 4], "float32"),
+    "qa": ("sbuf", [128, 2], "float32"),
     "qb": ("sbuf", [128, 2], "float32"),
     "ones": ("sbuf", [128, 128], "bfloat16"),
     "ident": ("sbuf", [128, 128], "bfloat16"),
@@ -28,10 +29,11 @@ SCRATCH = {
     "acc2": ("psum", [128, W], "float32"),
     "acc3": ("psum", [128, W], "float32"),
 }
-SEMAPHORES = (["el", "sent", "arr", "xl", "on", "pz", "idl", "xca", "xcb", "q", "q2", "yes", "sts", "sty"]
+SEMAPHORES = (["el", "sent", "arr", "xl", "on", "pz", "idl", "xca", "xcb", "q", "yes", "sts", "sty"]
               + ["tl%d" % k for k in range(5)]
-              + ["pr%d%d" % (k, h) for k in range(4) for h in range(2)]
-              + ["pl%d" % j for j in range(4)] + ["ad%d" % j for j in range(4)] + ["ev%d" % j for j in range(4)])
+              + ["pr%d%d" % (k, h) for k in range(2) for h in range(2)]
+              + ["pc%d%d" % (k, j) for k in range(2, 5) for j in range(4)]
+              + ["ad%d" % j for j in range(4)] + ["ev%d" % j for j in range(4)])
 
 
 def rank_program(g, core, T, topo):
@@ -91,67 +93,84 @@ def rank_program(g, core, T, topo):
     ve.memset(T.pb[:, 2 * W - 2:2 * W + 2], 0.0).then_inc(S.pz, 1)
     ve.memset(T.pb[:, 4 * W - 1:4 * W + 1], 0.0).then_inc(S.pz, 1)
 
-    def product(k, c0, c1, sem):
+    def product(k, c0, c1, sem, sbuf=False):
         d = ORDER[k] - R
         lo, hi = max(c0, -d), min(c1, W - d)
-        if c0 < HW_:
+        if sbuf:
+            xap = T.xs[:, lo + d:hi + d]
+        elif c0 < HW_:
             xap = T.xa[:, lo + d:hi + d]
         else:
             off = HW_ - R
             xap = T.xb[:, lo + d - off:hi + d - off]
         ve.tensor_tensor(T.pb[:, W * k + lo:W * k + hi], T.ts[:, W * k + lo:W * k + hi], xap, mult).then_inc(sem, 1)
 
+    ve.wait_ge(S.xl, 16)
+    ve.wait_ge(S.tl0, 16)
+    product(0, 0, FIRST, S.pr00, sbuf=True)
     ve.wait_ge(S.xca, 1)
-    for k in range(4):
-        ve.wait_ge(S["tl%d" % k], 16)
-        product(k, 0, HW_, S["pr%d0" % k])
-        if k == 0:
-            ve.wait_ge(S.xcb, 1)
-        product(k, HW_, W, S["pr%d1" % k])
-    ve.wait_ge(S.tl4, 16)
-    for j in LAST:
-        product(4, C * j, C * j + C, S["pl%d" % j])
+    product(0, FIRST, HW_, S.pr00)
+    ve.wait_ge(S.xcb, 1)
+    product(0, HW_, W, S.pr01)
+    ve.wait_ge(S.tl1, 16)
+    product(1, 0, HW_, S.pr10)
+    product(1, HW_, W, S.pr11)
+    for gi, grp in enumerate(GROUPS):
+        for k in range(2, 5):
+            if gi == 0:
+                ve.wait_ge(S["tl%d" % k], 16)
+            for j in grp:
+                product(k, C * j, C * j + C, S["pc%d%d" % (k, j)])
 
     pe.wait_ge(S.pz, 2)
-    for k in range(4):
+    for k in range(2):
         for h in range(2):
-            pe.wait_ge(S["pr%d%d" % (k, h)], 1)
+            pe.wait_ge(S["pr%d%d" % (k, h)], 2 if (k, h) == (0, 0) else 1)
             for j in (2 * h, 2 * h + 1):
                 pe.matmul(T["acc%d" % j][:, 0:C], T.ident[:], T.pb[:, W * k + C * j:W * k + C * j + C], k == 0, False)
-    for j in LAST:
-        pe.wait_ge(S["pl%d" % j], 1)
-        pe.matmul(T["acc%d" % j][:, 0:C], T.ident[:], T.pb[:, W * 4 + C * j:W * 4 + C * j + C], False,
-                  True).then_inc(S["ad%d" % j], 1)
+    for grp in GROUPS:
+        for k in range(2, 5):
+            for j in grp:
+                pe.wait_ge(S["pc%d%d" % (k, j)], 1)
+                mm = pe.matmul(T["acc%d" % j][:, 0:C], T.ident[:], T.pb[:, W * k + C * j:W * k + C * j + C], False,
+                               k == 4)
+                if k == 4:
+                    mm.then_inc(S["ad%d" % j], 1)
 
     def evacuate(j):
         sc.wait_ge(S["ad%d" % j], 1)
         sc.activation(T.ysb[:, ypos(j):ypos(j) + C], T["acc%d" % j][:, 0:C], copy).then_inc(S["ev%d" % j], 1)
 
     evacuate(3)
-    sc.wait_ge(S.ev3, 1)
-    sc.dma_start(T.y[:, 3 * C:W - R], T.ysb[:, ypos(3):ypos(3) + C - R]).then_inc(S.sts, 16)
     evacuate(0)
     evacuate(1)
-    sc.wait_ge(S.ev0, 1)
-    sc.wait_ge(S.ev1, 1)
-    sc.dma_start(T.y[:, R:2 * C], T.ysb[:, ypos(0) + R:ypos(0) + 2 * C]).then_inc(S.sts, 16)
     evacuate(2)
+    sy.wait_ge(S.ev3, 1)
+    sy.dma_start(T.y[:, 3 * C:W - R], T.ysb[:, ypos(3):ypos(3) + C - R]).then_inc(S.sty, 16)
+    sy.wait_ge(S.ev0, 1)
+    sy.dma_start(T.y[:, R:C], T.ysb[:, ypos(0) + R:ypos(0) + C]).then_inc(S.sty, 16)
+    sy.wait_ge(S.ev1, 1)
+    sy.dma_start(T.y[:, C:2 * C], T.ysb[:, ypos(1):ypos(1) + C]).then_inc(S.sty, 16)
     sc.wait_ge(S.ev2, 1)
     sc.dma_start(T.y[:, 2 * C:3 * C], T.ysb[:, ypos(2):ypos(2) + C]).then_inc(S.sts, 16)
 
+    e = HW_ - R
     ve.wait_ge(S.arr, 2 * NENG)
     ve.tensor_tensor(T.qb[:], T.ts[:, 4 * W - 1:4 * W + 1], T.hal8[:, 2:6:3], mult).then_inc(S.q, 1)
-    ve.tensor_tensor(T.qa[:], T.ts[:, 2 * W - 2:2 * W + 2], T.hal8[:, 2:6], mult).then_inc(S.q, 1)
-    ve.wait_ge(S.q, 2)
-    ve.tensor_tensor(T.qa[:, 1:3], T.qa[:, 1:3], T.qb[:], add).then_inc(S.q2, 1)
-    ve.wait_ge(S.q2, 1)
+    ve.tensor_tensor(T.qa[:], T.ts[:, 2 * W - 1:2 * W + 1], T.hal8[:, 3:5], mult).then_inc(S.q, 1)
     ve.wait_ge(S.ev3, 1)
     ve.wait_ge(S.ev0, 1)
-    ve.tensor_tensor(T.ye4[:], T.ysb[:, HW_ - R:HW_ + R], T.qa[:], add).then_inc(S.yes, 1)
+    ve.tensor_scalar(T.ye4[:, 0:1], T.hal8[:, 2:3], T.ts[:, 2 * W - 2:2 * W - 1], T.ysb[:, e:e + 1],
+                     mult, add).then_inc(S.yes, 1)
+    ve.tensor_scalar(T.ye4[:, 3:4], T.hal8[:, 5:6], T.ts[:, 2 * W + 1:2 * W + 2], T.ysb[:, e + 3:e + 4],
+                     mult, add).then_inc(S.yes, 1)
+    ve.wait_ge(S.q, 2)
+    ve.tensor_scalar(T.ye4[:, 1:2], T.ysb[:, e + 1:e + 2], T.qa[:, 0:1], T.qb[:, 0:1], add, add).then_inc(S.yes, 1)
+    ve.tensor_scalar(T.ye4[:, 2:3], T.ysb[:, e + 2:e + 3], T.qa[:, 1:2], T.qb[:, 1:2], add, add).then_inc(S.yes, 1)
 
-    sy.wait_ge(S.yes, 1)
+    sy.wait_ge(S.yes, 4)
     sy.dma_start(T.y[:, W - R:W], T.ye4[:, 0:R]).then_inc(S.sty, 16)
-    sc.wait_ge(S.yes, 1)
+    sc.wait_ge(S.yes, 4)
     sc.dma_start(T.y[:, 0:R], T.ye4[:, R:2 * R]).then_inc(S.sts, 16)
-    sy.wait_ge(S.sty, 16)
-    sc.wait_ge(S.sts, 64)
+    sy.wait_ge(S.sty, 64)
+    sc.wait_ge(S.sts, 32)

from concourse.bass import DstId, RemoteDMATransfer
from concourse.mybir import AluOpType, ActivationFunctionType

W = 512
HW_ = W // 2
C = W // 4
R = 2
NENG = 8
ORDER = [2, 4, 0, 3, 1]
FIRST = 160
GROUPS = [(3, 0), (1, 2)]

SCRATCH = {
    "eg": ("sbuf", [128, 4], "bfloat16"),
    "hal8": ("sbuf", [128, 8], "bfloat16"),
    "xs": ("sbuf", [128, W], "bfloat16"),
    "ts": ("sbuf", [128, 5 * W], "bfloat16"),
    "pb": ("sbuf", [128, 5 * W], "bfloat16"),
    "ysb": ("sbuf", [128, W], "bfloat16"),
    "ye4": ("sbuf", [128, 4], "bfloat16"),
    "qa": ("sbuf", [128, 2], "float32"),
    "qb": ("sbuf", [128, 2], "float32"),
    "ones": ("sbuf", [128, 128], "bfloat16"),
    "ident": ("sbuf", [128, 128], "bfloat16"),
    "xa": ("psum", [128, W], "float32"),
    "xb": ("psum", [128, W], "float32"),
    "acc0": ("psum", [128, W], "float32"),
    "acc1": ("psum", [128, W], "float32"),
    "acc2": ("psum", [128, W], "float32"),
    "acc3": ("psum", [128, W], "float32"),
}
SEMAPHORES = (["el", "sent", "arr", "xl", "on", "pz", "idl", "xca", "xcb", "q", "yes", "sts", "sty"]
              + ["tl%d" % k for k in range(5)]
              + ["pr%d%d" % (k, h) for k in range(2) for h in range(2)]
              + ["pc%d%d" % (k, j) for k in range(2, 5) for j in range(4)]
              + ["ad%d" % j for j in range(4)] + ["ev%d" % j for j in range(4)])


def rank_program(g, core, T, topo):
    rank = T.rank_of(core)
    if rank is None:
        return
    n = len(T.cores)
    left, right = T.cores[(rank - 1) % n], T.cores[(rank + 1) % n]
    S = T.sem
    sy, sc, ve, pe = g.sync, g.scalar, g.vector, g.tensor
    mult, add = AluOpType.mult, AluOpType.add
    copy = ActivationFunctionType.Copy

    def load_table(q, k):
        i = ORDER[k]
        q.dma_start(T.ts[:, W * k:W * k + W], T.t[:, W * i:W * i + W]).then_inc(S["tl%d" % k], 16)

    def ypos(j):
        return (C * j + HW_) % W

    sy.dma_start(T.eg[:, 2:4], T.x[:, 0:2]).then_inc(S.el, 16)
    sc.dma_start(T.eg[:, 0:2], T.x[:, W - 2:W]).then_inc(S.el, 16)
    sy.dma_start(T.xs[:], T.x[:]).then_inc(S.xl, 16)
    load_table(sc, 0)
    load_table(sy, 1)
    load_table(sc, 2)
    load_table(sy, 3)
    load_table(sc, 4)

    g.wait_ge(S.on, 1)
    g.affine_select(T.ident[:], T.ones[:], [[-1, 128]], AluOpType.is_equal, 0.0, 0, 1).then_inc(S.idl, 1)
    g.wait_ge(S.el, 32)
    dests = [(left, T.hal8[:, 0:4]), (right, T.hal8[:, 4:8])]
    here = (topo.host(core), topo.chip(core))
    dests.sort(key=lambda d: (topo.host(d[0]), topo.chip(d[0])) == here)
    allowed = topo.mask(core, left) & topo.mask(core, right)
    engines = 0
    for _ in range(NENG):
        rest = allowed & ~engines
        engines |= rest & (-rest)
    ids = []
    for d, _ in dests:
        rid, pid = topo.addr(d, core)
        ids.append(DstId(rid=rid, pnc=pid))
    g.remote_dma_fused([RemoteDMATransfer(dst_ids=ids, dma_engine_mask=engines, remote_sem=S.arr,
                                          srcs=[T.eg[:]], dsts=[ap for _, ap in dests], alu_op=0)],
                       local_sem=S.sent)
    g.wait_ge(S.sent, NENG)

    pe.wait_ge(S.idl, 1)
    pe.wait_ge(S.xl, 16)
    pe.matmul(T.xa[:, 0:HW_ + R], T.ident[:], T.xs[:, 0:HW_ + R], True, True).then_inc(S.xca, 1)
    sc.wait_ge(S.xl, 16)
    sc.activation(T.xb[:, 0:HW_ + R], T.xs[:, HW_ - R:W], copy).then_inc(S.xcb, 1)

    ve.memset(T.ones[:], 1.0).then_inc(S.on, 1)
    ve.memset(T.pb[:, 2 * W - 2:2 * W + 2], 0.0).then_inc(S.pz, 1)
    ve.memset(T.pb[:, 4 * W - 1:4 * W + 1], 0.0).then_inc(S.pz, 1)

    def product(k, c0, c1, sem, sbuf=False):
        d = ORDER[k] - R
        lo, hi = max(c0, -d), min(c1, W - d)
        if sbuf:
            xap = T.xs[:, lo + d:hi + d]
        elif c0 < HW_:
            xap = T.xa[:, lo + d:hi + d]
        else:
            off = HW_ - R
            xap = T.xb[:, lo + d - off:hi + d - off]
        ve.tensor_tensor(T.pb[:, W * k + lo:W * k + hi], T.ts[:, W * k + lo:W * k + hi], xap, mult).then_inc(sem, 1)

    ve.wait_ge(S.xl, 16)
    ve.wait_ge(S.tl0, 16)
    product(0, 0, FIRST, S.pr00, sbuf=True)
    ve.wait_ge(S.xca, 1)
    product(0, FIRST, HW_, S.pr00)
    ve.wait_ge(S.xcb, 1)
    product(0, HW_, W, S.pr01)
    ve.wait_ge(S.tl1, 16)
    product(1, 0, HW_, S.pr10)
    product(1, HW_, W, S.pr11)
    for gi, grp in enumerate(GROUPS):
        for k in range(2, 5):
            if gi == 0:
                ve.wait_ge(S["tl%d" % k], 16)
            for j in grp:
                product(k, C * j, C * j + C, S["pc%d%d" % (k, j)])

    pe.wait_ge(S.pz, 2)
    for k in range(2):
        for h in range(2):
            pe.wait_ge(S["pr%d%d" % (k, h)], 2 if (k, h) == (0, 0) else 1)
            for j in (2 * h, 2 * h + 1):
                pe.matmul(T["acc%d" % j][:, 0:C], T.ident[:], T.pb[:, W * k + C * j:W * k + C * j + C], k == 0, False)
    for grp in GROUPS:
        for k in range(2, 5):
            for j in grp:
                pe.wait_ge(S["pc%d%d" % (k, j)], 1)
                mm = pe.matmul(T["acc%d" % j][:, 0:C], T.ident[:], T.pb[:, W * k + C * j:W * k + C * j + C], False,
                               k == 4)
                if k == 4:
                    mm.then_inc(S["ad%d" % j], 1)

    def evacuate(j):
        sc.wait_ge(S["ad%d" % j], 1)
        sc.activation(T.ysb[:, ypos(j):ypos(j) + C], T["acc%d" % j][:, 0:C], copy).then_inc(S["ev%d" % j], 1)

    evacuate(3)
    evacuate(0)
    evacuate(1)
    evacuate(2)
    sy.wait_ge(S.ev3, 1)
    sy.dma_start(T.y[:, 3 * C:W - R], T.ysb[:, ypos(3):ypos(3) + C - R]).then_inc(S.sty, 16)
    sy.wait_ge(S.ev0, 1)
    sy.dma_start(T.y[:, R:C], T.ysb[:, ypos(0) + R:ypos(0) + C]).then_inc(S.sty, 16)
    sy.wait_ge(S.ev1, 1)
    sy.dma_start(T.y[:, C:2 * C], T.ysb[:, ypos(1):ypos(1) + C]).then_inc(S.sty, 16)
    sc.wait_ge(S.ev2, 1)
    sc.dma_start(T.y[:, 2 * C:3 * C], T.ysb[:, ypos(2):ypos(2) + C]).then_inc(S.sts, 16)

    e = HW_ - R
    ve.wait_ge(S.arr, 2 * NENG)
    ve.tensor_tensor(T.qb[:], T.ts[:, 4 * W - 1:4 * W + 1], T.hal8[:, 2:6:3], mult).then_inc(S.q, 1)
    ve.tensor_tensor(T.qa[:], T.ts[:, 2 * W - 1:2 * W + 1], T.hal8[:, 3:5], mult).then_inc(S.q, 1)
    ve.wait_ge(S.ev3, 1)
    ve.wait_ge(S.ev0, 1)
    ve.tensor_scalar(T.ye4[:, 0:1], T.hal8[:, 2:3], T.ts[:, 2 * W - 2:2 * W - 1], T.ysb[:, e:e + 1],
                     mult, add).then_inc(S.yes, 1)
    ve.tensor_scalar(T.ye4[:, 3:4], T.hal8[:, 5:6], T.ts[:, 2 * W + 1:2 * W + 2], T.ysb[:, e + 3:e + 4],
                     mult, add).then_inc(S.yes, 1)
    ve.wait_ge(S.q, 2)
    ve.tensor_scalar(T.ye4[:, 1:2], T.ysb[:, e + 1:e + 2], T.qa[:, 0:1], T.qb[:, 0:1], add, add).then_inc(S.yes, 1)
    ve.tensor_scalar(T.ye4[:, 2:3], T.ysb[:, e + 2:e + 3], T.qa[:, 1:2], T.qb[:, 1:2], add, add).then_inc(S.yes, 1)

    sy.wait_ge(S.yes, 4)
    sy.dma_start(T.y[:, W - R:W], T.ye4[:, 0:R]).then_inc(S.sty, 16)
    sc.wait_ge(S.yes, 4)
    sc.dma_start(T.y[:, 0:R], T.ye4[:, R:2 * R]).then_inc(S.sts, 16)
    sy.wait_ge(S.sty, 64)
    sc.wait_ge(S.sts, 32)
